import numpy as np
import ml_dtypes


def mxq(x, axis, fmt="e4m3"):
    dtype, down = {"e4m3": (ml_dtypes.float8_e4m3fn, 7), "e5m2": (ml_dtypes.float8_e5m2, 14)}[fmt]
    v = np.moveaxis(np.asarray(x, np.float32).astype(ml_dtypes.bfloat16).astype(np.float64), axis, -1)
    blocks = v.reshape(v.shape[:-1] + (-1, 32))
    amax = np.abs(blocks).max(-1, keepdims=True)
    byte = np.maximum(np.where(amax > 0, np.frexp(amax)[1] - 1 + 127, 0) - down, 1)
    scale = np.exp2(byte - 127.0)
    codes = (blocks / scale).astype(np.float32).astype(dtype).astype(np.float64)
    return np.moveaxis((codes * scale).reshape(v.shape), -1, axis)


WIDE = False


def mx_kscale(k):
    if not WIDE:
        return np.ones(k)
    levels = np.array([10, -10, 5, -5, 0])
    if k % 512:
        return np.exp2(np.random.permutation(np.resize(levels, k // 32))).repeat(32)
    a = np.empty((k // 512, 16))
    for p in range(k // 512):
        a[p, :8] = np.random.permutation(np.resize(levels, 8))
        for g in range(8):
            far = levels[np.abs(levels - a[p, g]) >= 10]
            a[p, g + 8] = far[np.random.randint(len(far))]
    return np.exp2(a.ravel()).repeat(32)


def f64(x):
    return np.asarray(x).astype(np.float64)


def striped(idx):
    return np.tile(idx.reshape(-1, 16).T, (8, 1)).astype(np.uint16)


def unstriped(offs):
    return offs[:16].T.reshape(-1).astype(np.int64)


def striped8(idx):
    return np.concatenate([x.reshape(-1, 16).T for x in idx]).astype(np.uint16)


def runs(offs, k):
    lists = np.stack([offs[16 * r : 16 * r + 16].T.reshape(-1) for r in range(8)]).astype(np.int64)
    return lists[np.arange(k) % 512 // 64]


def pack_weight(w):
    k, n = w.shape
    w = f64(np.asarray(w, np.float32).astype(ml_dtypes.bfloat16)).reshape(k // 32, 32, n)
    amax = np.abs(w).max(1)
    byte = np.clip(np.where(amax > 0, np.frexp(amax)[1] - 1 + 127 - 7, 1), 1, 254)
    scaled = (w * np.exp2(127.0 - byte)[:, None, :]).reshape(k, n).astype(np.float32)
    words = np.ascontiguousarray(scaled.reshape(k // 512, 128, 4, n).transpose(0, 1, 3, 2)).astype(ml_dtypes.float8_e4m3fn).view(np.uint8)
    return words, np.ascontiguousarray(byte.astype(np.uint8).reshape(k // 512, 16, n))


def unpack_weight(words, scales):
    g, p, n, _ = words.shape
    vals = np.ascontiguousarray(words).view(ml_dtypes.float8_e4m3fn).astype(np.float64) * np.repeat(np.exp2(scales.astype(np.float64) - 127.0), 8, axis=1)[..., None]
    return vals.transpose(0, 1, 3, 2).reshape(g * 512, n)


K, T, S, H, G = 512, 1024, 512, 512, 2048


def setup_inputs():
    n = np.random.standard_normal
    s = mx_kscale(K)[:, None]
    packed_xT = pack_weight(n((K, T)) * s)
    packed_dT = pack_weight(n((K, G)) / s)
    return {
        "x_words": packed_xT[0],
        "x_scales": packed_xT[1],
        "w1": (n((K, H)) / np.sqrt(K) / s).astype(np.float32),
        "w2": (n((K, H)) / np.sqrt(K) / s).astype(np.float32),
        "gs": (np.random.uniform(0.5, 1.5, (K, 1)) * s).astype(np.float32),
        "d_words": packed_dT[0],
        "d_scales": packed_dT[1],
        "tau": np.random.uniform(0.3, 0.9, (H, 1)).astype(np.float32),
        "offs": striped(np.random.permutation(T)[:S]),
        "two": striped(np.random.permutation(T)[:S]),
        "n1": striped(np.random.permutation(S)),
        "n2": striped(np.random.permutation(S)),
        "n3": striped(np.random.permutation(S)),
        "k1": striped8(np.random.randint(0, G, (8, H))),
        "n4": striped8(np.stack([np.random.permutation(S) for _ in range(8)])),
        "n5": striped8(np.stack([np.random.permutation(S) for _ in range(8)])),
    }


def reference(x_words, x_scales, w1, w2, gs, d_words, d_scales, tau, offs, two, n1, n2, n3, k1, n4, n5):
    d_k1 = unpack_weight(d_words, d_scales)[np.arange(K)[:, None], runs(k1, K)]
    xq = unpack_weight(x_words, x_scales)[:, unstriped(offs)]
    y = mxq(f64(w1), 0, "e4m3").T @ xq
    x_two = unpack_weight(x_words, x_scales)[:, unstriped(two)]
    d = mxq(f64(w2), 0, "e4m3").T @ x_two
    z = f64(gs) * (np.maximum(np.minimum(y - (0.5 * y[:, unstriped(n1)]), d[:, unstriped(n2)]), d[:, unstriped(n3)]))
    h = 0.0625 * ((d_k1.T @ mxq(z, 0, "e4m3")))
    low = h.min(axis=1, keepdims=True)
    ea = np.exp(f64(tau) * (low - (h[np.arange(H)[:, None], runs(n4, H)])))
    return h - (2.0 * (ea * (h[np.arange(H)[:, None], runs(n5, H)])))

@@ -1,0 +1,213 @@
+from contextlib import ExitStack
+
+import concourse.mybir as mybir
+
+FLOPS = 805306368
+
+F32 = mybir.dt.float32
+BF16 = mybir.dt.bfloat16
+I32 = mybir.dt.int32
+U32 = mybir.dt.uint32
+U16 = mybir.dt.uint16
+U8 = mybir.dt.uint8
+FP8X4 = mybir.dt.float8_e4m3fn_x4
+ALU = mybir.AluOpType
+ACT = mybir.ActivationFunctionType
+
+P = 128
+PACK = 4
+S = 512
+T = 1024
+G = 2048
+HALF = S // 2
+LIST_COLS = S // 16
+
+
+def tile_picked_twqclampbebz_none_p_kernel(
+    tc, x_words, x_scales, w1, w2, gs, d_words, d_scales, tau, offs, two, n1, n2, n3, k1, n4, n5, out
+):
+    nc = tc.nc
+    with ExitStack() as ctx:
+        sb = ctx.enter_context(tc.tile_pool(name="sb", bufs=1))
+        ps = ctx.enter_context(tc.psum_pool(name="ps", bufs=1))
+
+        def sbuf(name, shape, dtype):
+            return sb.tile(shape, dtype, name=name, align_bytes=64)
+
+        def load_list(name, src):
+            lst = sbuf(name, [P, LIST_COLS], U16)
+            nc.sync.dma_start(lst[:], src)
+            return lst
+
+        def half_cols(h):
+            return slice(h * HALF, (h + 1) * HALF)
+
+        def half_list(lst, h):
+            return lst[:, h * LIST_COLS // 2 : (h + 1) * LIST_COLS // 2]
+
+        def load_weight_half(name, w, h):
+            raw = sbuf(name, [P, PACK, HALF], F32)
+            nc.sync.dma_start(raw[:], w.rearrange("(p j) c -> p j c", j=PACK)[:, :, half_cols(h)])
+            return raw
+
+        xs_tab = sbuf("xs_tab", [P, T], U8)
+        ds_tab = sbuf("ds_tab", [P, G], U8)
+        nc.vector.memset(xs_tab[:].bitcast(I32), 0)
+        nc.gpsimd.memset(ds_tab[:].bitcast(I32), 0)
+
+        offs_l = load_list("offs_l", offs)
+        xw_tab = sbuf("xw_tab", [P, T], U32)
+        nc.sync.dma_start(xw_tab[:].bitcast(I32), x_words[0].rearrange("p n r -> p (n r)").bitcast(I32))
+        for q in range(4):
+            nc.scalar.dma_start(
+                xs_tab[:].bitcast(I32)[32 * q : 32 * q + 4, :], x_scales[0].bitcast(I32)[4 * q : 4 * q + 4, :]
+            )
+        w1_raw = [load_weight_half("w1_raw%d" % h, w1, h) for h in range(2)]
+        two_l = load_list("two_l", two)
+        w2_raw = [load_weight_half("w2_raw%d" % h, w2, h) for h in range(2)]
+        n1_l = load_list("n1_l", n1)
+        n2_l = load_list("n2_l", n2)
+        n3_l = load_list("n3_l", n3)
+        k1_l = load_list("k1_l", k1)
+        for e in range(2):
+            nc.sync.dma_start(ds_tab[:].bitcast(I32)[e:P:16, :], d_scales[0].bitcast(I32)[e:16:2, :])
+        dw_tab = sbuf("dw_tab", [P, G], U32)
+        nc.sync.dma_start(dw_tab[:].bitcast(I32), d_words[0].rearrange("p n r -> p (n r)").bitcast(I32))
+        gs_t = sbuf("gs_t", [P, PACK], F32)
+        nc.sync.dma_start(gs_t[:], gs.rearrange("(p t) o -> p (t o)", t=PACK))
+        tau_t = sbuf("tau_t", [P, PACK], F32)
+        nc.sync.dma_start(tau_t[:], tau.rearrange("(p t) o -> p (t o)", t=PACK))
+        n4_l = load_list("n4_l", n4)
+        n5_l = load_list("n5_l", n5)
+
+        def gather_packed(name, lst):
+            words = sbuf(name + "_words", [P, S], U32)
+            nc.vector.tensor_copy(words[:], xw_tab[:].indirect(lst[:]))
+            scales = sbuf(name + "_scales", [P, S], U8)
+            nc.vector.tensor_copy(scales[:], xs_tab[:].indirect(lst[:]))
+            return words, scales
+
+        def round_weight(name, raw):
+            dealt = sbuf(name, [P, PACK, P, PACK], BF16)
+            for h in range(2):
+                nc.scalar.copy(
+                    dealt[:, :, h * P // 2 : (h + 1) * P // 2, :].rearrange("p t m j -> p m j t"),
+                    raw[h][:].rearrange("p j (m t) -> p m j t", t=PACK),
+                )
+            return dealt
+
+        def quantize(name, values, width):
+            words = sbuf(name + "_words", [P, width], U32)
+            scales = sbuf(name + "_scales", [P, width], U8)
+            nc.vector.quantize_mx(out=words[:].bitcast(FP8X4), scales=scales[:], in_=values)
+            return words, scales
+
+        def product(acc, stat, t, mov):
+            cols = slice(t * P, (t + 1) * P)
+            nc.tensor.matmul_mx(
+                out=acc,
+                lhsT=stat[0][:, cols].bitcast(FP8X4),
+                lhsT_scale=stat[1][:, cols],
+                rhs=mov[0][:].bitcast(FP8X4),
+                rhs_scale=mov[1][:],
+                start=True,
+                stop=True,
+            )
+
+        w1_bf = round_weight("w1_bf", w1_raw)
+        w2_bf = round_weight("w2_bf", w2_raw)
+
+        xq = gather_packed("xq", offs_l)
+        w1_q = quantize("w1_q", w1_bf[:].rearrange("p t m j -> p (t m j)"), S)
+        x2 = gather_packed("x2", two_l)
+        y_ps, y_win = [], []
+        for t in range(PACK):
+            acc = ps.tile([P, S], F32, name="y_ps%d" % t)
+            product(acc[:], w1_q, t, xq)
+            win = sbuf("y_win%d" % t, [P, S], F32)
+            nc.vector.tensor_copy(win[:], acc[:])
+            y_ps.append(acc)
+            y_win.append(win)
+        w2_q = quantize("w2_q", w2_bf[:].rearrange("p t m j -> p (t m j)"), S)
+        d_win = []
+        for t in range(PACK):
+            acc = ps.tile([P, S], F32, name="d_ps%d" % t, tag="bank%d" % t)
+            product(acc[:], w2_q, t, x2)
+            win = sbuf("d_win%d" % t, [P, S], F32)
+            if t % 2 == 0:
+                nc.vector.tensor_copy(win[:], acc[:])
+            else:
+                nc.scalar.copy(win[:], acc[:])
+            d_win.append(win)
+
+        dk_bytes = sbuf("dk_bytes", [P, S], U8)
+        nc.vector.tensor_copy(dk_bytes[:], ds_tab[:].indirect(k1_l[:]))
+        dk_scales = sbuf("dk_scales", [P, S], U8)
+        nc.vector.tensor_copy(
+            dk_scales[:].rearrange("p (t m) -> p m t", t=PACK), dk_bytes[:].rearrange("p (m t) -> p m t", t=PACK)
+        )
+        for e in range(2):
+            nc.sync.dma_start(dk_scales[:].bitcast(I32)[2 + e : P : 32, :], dk_scales[:].bitcast(I32)[16 + e : P : 32, :])
+        dk_picked = sbuf("dk_picked", [P, S], U32)
+        nc.vector.tensor_copy(dk_picked[:], dw_tab[:].indirect(k1_l[:]))
+        dk_words = sbuf("dk_words", [P, S], U32)
+        nc.vector.tensor_copy(
+            dk_words[:].rearrange("p (t m) -> p m t", t=PACK), dk_picked[:].rearrange("p (m t) -> p m t", t=PACK)
+        )
+        neg_tau = sbuf("neg_tau", [P, PACK], F32)
+        nc.vector.tensor_scalar(neg_tau[:], tau_t[:], -1.0, None, ALU.mult)
+
+        h_ps = [ps.tile([P, S], F32, name="h_ps%d" % t, tag="bank%d" % t) for t in range(PACK)]
+        h_win = [sbuf("h_win%d" % t, [P, S], F32) for t in range(PACK)]
+        lows = [[sbuf("low%d_%d" % (h, t), [P, 1], F32) for t in range(PACK)] for h in range(2)]
+        for h in range(2):
+            clamped = sbuf("clamped%d" % h, [P, PACK, HALF], F32)
+            for t in range(PACK):
+                fetched = []
+                for nm, win, lst in (("y1", y_win[t], n1_l), ("d2", d_win[t], n2_l), ("d3", d_win[t], n3_l)):
+                    got = sbuf("%s_%d_%d" % (nm, h, t), [P, HALF], F32)
+                    nc.scalar.activation(got[:], win[:].indirect(half_list(lst, h)), ACT.Copy)
+                    fetched.append(got)
+                diff = sbuf("diff_%d_%d" % (h, t), [P, HALF], F32)
+                nc.vector.scalar_tensor_tensor(
+                    diff[:], fetched[0][:], -0.5, y_ps[t][:, half_cols(h)], ALU.mult, ALU.add
+                )
+                lesser = sbuf("lesser_%d_%d" % (h, t), [P, HALF], F32)
+                nc.vector.tensor_tensor(lesser[:], diff[:], fetched[1][:], ALU.min)
+                nc.vector.tensor_tensor(clamped[:, t, :], lesser[:], fetched[2][:], ALU.max)
+            z_bf = sbuf("z_bf%d" % h, [P, HALF, PACK], BF16)
+            nc.vector.tensor_tensor(
+                z_bf[:].rearrange("p (c i) t -> p c t i", i=4),
+                clamped[:].rearrange("p t (c i) -> p c t i", i=4),
+                gs_t[:].unsqueeze(1).unsqueeze(3).to_broadcast([P, HALF // 4, PACK, 4]),
+                ALU.mult,
+            )
+            z_q = quantize("z_q%d" % h, z_bf[:].rearrange("p c t -> p (c t)"), HALF)
+            for t in range(PACK):
+                product(h_ps[t][:, half_cols(h)], (dk_words, dk_scales), t, z_q)
+                nc.vector.tensor_scalar(
+                    h_win[t][:, half_cols(h)],
+                    h_ps[t][:, half_cols(h)],
+                    0.0625,
+                    lows[0][t][:] if h == 1 else None,
+                    ALU.mult,
+                    ALU.min,
+                    accum_out=lows[h][t][:],
+                )
+
+        out_rows = out.rearrange("(p t) c -> t p c", t=PACK)
+        for t in range(PACK):
+            bias = sbuf("bias%d" % t, [P, 1], F32)
+            nc.scalar.activation(bias[:], lows[1][t][:], ACT.Copy, scale=tau_t[:, t : t + 1])
+            for h in range(2):
+                ea = sbuf("ea_%d_%d" % (t, h), [P, HALF], F32)
+                nc.scalar.activation(
+                    ea[:], h_win[t][:].indirect(half_list(n4_l, h)), ACT.Exp, bias=bias[:], scale=neg_tau[:, t : t + 1]
+                )
+                prod = sbuf("prod_%d_%d" % (t, h), [P, HALF], F32)
+                nc.vector.tensor_tensor(prod[:], h_win[t][:].indirect(half_list(n5_l, h)), ea[:], ALU.mult)
+                res = sbuf("res_%d_%d" % (t, h), [P, HALF], F32)
+                nc.vector.scalar_tensor_tensor(
+                    res[:], prod[:], -2.0, h_win[t][:, half_cols(h)], ALU.mult, ALU.add
+                )
+                nc.sync.dma_start(out_rows[t][:, half_cols(h)], res[:])

@@ -20,6 +20,10 @@ S = 512
 T = 1024
 G = 2048
 HALF = S // 2
+CHUNKS = ((0, 256), (256, 512))
+MM_PIECES = (((0, 256),), ((256, 384), (384, 512)))
+Y_EVAC_ON_VECTOR = (1, 2)
+N5_ON_SCALAR = ((2, 1), (3, 0), (3, 1))
 LIST_COLS = S // 16
 
 
@@ -29,10 +33,14 @@ def tile_picked_twqclampbebz_none_p_kernel(
     nc = tc.nc
     with ExitStack() as ctx:
         sb = ctx.enter_context(tc.tile_pool(name="sb", bufs=1))
+        rot = ctx.enter_context(tc.tile_pool(name="rot", bufs=2))
         ps = ctx.enter_context(tc.psum_pool(name="ps", bufs=1))
 
-        def sbuf(name, shape, dtype):
-            return sb.tile(shape, dtype, name=name, align_bytes=64)
+        def sbuf(name, shape, dtype, tag=None):
+            return sb.tile(shape, dtype, name=name, tag=tag or name, align_bytes=64)
+
+        def rotating(name, shape, dtype, tag):
+            return rot.tile(shape, dtype, name=name, tag=tag, align_bytes=64)
 
         def load_list(name, src):
             lst = sbuf(name, [P, LIST_COLS], U16)
@@ -52,22 +60,22 @@ def tile_picked_twqclampbebz_none_p_kernel(
 
         xs_tab = sbuf("xs_tab", [P, T], U8)
         ds_tab = sbuf("ds_tab", [P, G], U8)
-        nc.vector.memset(xs_tab[:].bitcast(I32), 0)
+        nc.gpsimd.memset(xs_tab[:].bitcast(I32), 0)
         nc.gpsimd.memset(ds_tab[:].bitcast(I32), 0)
 
         offs_l = load_list("offs_l", offs)
         xw_tab = sbuf("xw_tab", [P, T], U32)
         nc.sync.dma_start(xw_tab[:].bitcast(I32), x_words[0].rearrange("p n r -> p (n r)").bitcast(I32))
         for q in range(4):
-            nc.scalar.dma_start(
+            nc.sync.dma_start(
                 xs_tab[:].bitcast(I32)[32 * q : 32 * q + 4, :], x_scales[0].bitcast(I32)[4 * q : 4 * q + 4, :]
             )
-        w1_raw = [load_weight_half("w1_raw%d" % h, w1, h) for h in range(2)]
         two_l = load_list("two_l", two)
-        w2_raw = [load_weight_half("w2_raw%d" % h, w2, h) for h in range(2)]
+        w1_raw = [load_weight_half("w1_raw%d" % h, w1, h) for h in range(2)]
         n1_l = load_list("n1_l", n1)
         n2_l = load_list("n2_l", n2)
         n3_l = load_list("n3_l", n3)
+        w2_raw = [load_weight_half("w2_raw%d" % h, w2, h) for h in range(2)]
         k1_l = load_list("k1_l", k1)
         for e in range(2):
             nc.sync.dma_start(ds_tab[:].bitcast(I32)[e:P:16, :], d_scales[0].bitcast(I32)[e:16:2, :])
@@ -80,10 +88,10 @@ def tile_picked_twqclampbebz_none_p_kernel(
         n4_l = load_list("n4_l", n4)
         n5_l = load_list("n5_l", n5)
 
-        def gather_packed(name, lst):
+        def gather_packed(name, lst, scales_tag=None):
             words = sbuf(name + "_words", [P, S], U32)
             nc.vector.tensor_copy(words[:], xw_tab[:].indirect(lst[:]))
-            scales = sbuf(name + "_scales", [P, S], U8)
+            scales = sbuf(name + "_scales", [P, S], U8, tag=scales_tag)
             nc.vector.tensor_copy(scales[:], xs_tab[:].indirect(lst[:]))
             return words, scales
 
@@ -102,14 +110,14 @@ def tile_picked_twqclampbebz_none_p_kernel(
             nc.vector.quantize_mx(out=words[:].bitcast(FP8X4), scales=scales[:], in_=values)
             return words, scales
 
-        def product(acc, stat, t, mov):
+        def product(acc, stat, t, mov, mcols=slice(0, S)):
             cols = slice(t * P, (t + 1) * P)
             nc.tensor.matmul_mx(
                 out=acc,
                 lhsT=stat[0][:, cols].bitcast(FP8X4),
                 lhsT_scale=stat[1][:, cols],
-                rhs=mov[0][:].bitcast(FP8X4),
-                rhs_scale=mov[1][:],
+                rhs=mov[0][:, mcols].bitcast(FP8X4),
+                rhs_scale=mov[1][:, mcols],
                 start=True,
                 stop=True,
             )
@@ -119,28 +127,29 @@ def tile_picked_twqclampbebz_none_p_kernel(
 
         xq = gather_packed("xq", offs_l)
         w1_q = quantize("w1_q", w1_bf[:].rearrange("p t m j -> p (t m j)"), S)
-        x2 = gather_packed("x2", two_l)
+        x2 = gather_packed("x2", two_l, scales_tag="w1_bf")
         y_ps, y_win = [], []
         for t in range(PACK):
             acc = ps.tile([P, S], F32, name="y_ps%d" % t)
             product(acc[:], w1_q, t, xq)
-            win = sbuf("y_win%d" % t, [P, S], F32)
-            nc.vector.tensor_copy(win[:], acc[:])
             y_ps.append(acc)
-            y_win.append(win)
-        w2_q = quantize("w2_q", w2_bf[:].rearrange("p t m j -> p (t m j)"), S)
-        d_win = []
-        for t in range(PACK):
-            acc = ps.tile([P, S], F32, name="d_ps%d" % t, tag="bank%d" % t)
-            product(acc[:], w2_q, t, x2)
-            win = sbuf("d_win%d" % t, [P, S], F32)
-            if t % 2 == 0:
+            if t == 3:
+                continue
+            win = sbuf("y_win%d" % t, [P, S], F32, tag="w2_raw1" if t == 0 else None)
+            if t in Y_EVAC_ON_VECTOR:
                 nc.vector.tensor_copy(win[:], acc[:])
             else:
                 nc.scalar.copy(win[:], acc[:])
-            d_win.append(win)
+            y_win.append(win)
+        w2_q = quantize("w2_q", w2_bf[:].rearrange("p t m j -> p (t m j)"), S)
+        d_ps, d_win = [], []
+        for t in range(PACK):
+            acc = ps.tile([P, S], F32, name="d_ps%d" % t, tag="bank%d" % t)
+            product(acc[:], w2_q, t, x2)
+            d_ps.append(acc)
+            d_win.append(sbuf("d_win%d" % t, [P, S], F32))
 
-        dk_bytes = sbuf("dk_bytes", [P, S], U8)
+        dk_bytes = rotating("dk_bytes", [P, S], U8, "lesser")
         nc.vector.tensor_copy(dk_bytes[:], ds_tab[:].indirect(k1_l[:]))
         dk_scales = sbuf("dk_scales", [P, S], U8)
         nc.vector.tensor_copy(
@@ -148,7 +157,7 @@ def tile_picked_twqclampbebz_none_p_kernel(
         )
         for e in range(2):
             nc.sync.dma_start(dk_scales[:].bitcast(I32)[2 + e : P : 32, :], dk_scales[:].bitcast(I32)[16 + e : P : 32, :])
-        dk_picked = sbuf("dk_picked", [P, S], U32)
+        dk_picked = rotating("dk_picked", [P, S], U32, "lesser")
         nc.vector.tensor_copy(dk_picked[:], dw_tab[:].indirect(k1_l[:]))
         dk_words = sbuf("dk_words", [P, S], U32)
         nc.vector.tensor_copy(
@@ -157,57 +166,83 @@ def tile_picked_twqclampbebz_none_p_kernel(
         neg_tau = sbuf("neg_tau", [P, PACK], F32)
         nc.vector.tensor_scalar(neg_tau[:], tau_t[:], -1.0, None, ALU.mult)
 
-        h_ps = [ps.tile([P, S], F32, name="h_ps%d" % t, tag="bank%d" % t) for t in range(PACK)]
+        h_ps = []
         h_win = [sbuf("h_win%d" % t, [P, S], F32) for t in range(PACK)]
-        lows = [[sbuf("low%d_%d" % (h, t), [P, 1], F32) for t in range(PACK)] for h in range(2)]
-        for h in range(2):
-            clamped = sbuf("clamped%d" % h, [P, PACK, HALF], F32)
+        lows = [sbuf("low%d" % h, [P, PACK], F32) for h in range(2)]
+        for h, (c0, c1) in enumerate(CHUNKS):
+            width = c1 - c0
+            clamped = sbuf("clamped%d" % h, [P, PACK, width], F32)
+            pending = None
             for t in range(PACK):
+                if h == 0:
+                    if t == 3:
+                        y_win.append(sbuf("y_win3", [P, S], F32, tag="w2_bf"))
+                        nc.scalar.copy(y_win[3][:], y_ps[3][:])
+                    nc.scalar.copy(d_win[t][:], d_ps[t][:])
                 fetched = []
                 for nm, win, lst in (("y1", y_win[t], n1_l), ("d2", d_win[t], n2_l), ("d3", d_win[t], n3_l)):
-                    got = sbuf("%s_%d_%d" % (nm, h, t), [P, HALF], F32)
-                    nc.scalar.activation(got[:], win[:].indirect(half_list(lst, h)), ACT.Copy)
+                    got = sbuf("%s_%d_%d" % (nm, h, t), [P, width], F32, tag="%s_%d" % (nm, t))
+                    nc.scalar.activation(got[:], win[:].indirect(lst[:, c0 // 16 : c1 // 16]), ACT.Copy)
                     fetched.append(got)
-                diff = sbuf("diff_%d_%d" % (h, t), [P, HALF], F32)
-                nc.vector.scalar_tensor_tensor(
-                    diff[:], fetched[0][:], -0.5, y_ps[t][:, half_cols(h)], ALU.mult, ALU.add
-                )
-                lesser = sbuf("lesser_%d_%d" % (h, t), [P, HALF], F32)
+                diff = rotating("diff_%d_%d" % (h, t), [P, width], F32, "diff")
+                nc.vector.scalar_tensor_tensor(diff[:], fetched[0][:], -0.5, y_ps[t][:, c0:c1], ALU.mult, ALU.add)
+                if pending is not None:
+                    nc.vector.tensor_tensor(*pending, ALU.max)
+                lesser = rotating("lesser_%d_%d" % (h, t), [P, width], F32, "lesser")
                 nc.vector.tensor_tensor(lesser[:], diff[:], fetched[1][:], ALU.min)
-                nc.vector.tensor_tensor(clamped[:, t, :], lesser[:], fetched[2][:], ALU.max)
-            z_bf = sbuf("z_bf%d" % h, [P, HALF, PACK], BF16)
-            nc.vector.tensor_tensor(
-                z_bf[:].rearrange("p (c i) t -> p c t i", i=4),
-                clamped[:].rearrange("p t (c i) -> p c t i", i=4),
-                gs_t[:].unsqueeze(1).unsqueeze(3).to_broadcast([P, HALF // 4, PACK, 4]),
-                ALU.mult,
-            )
-            z_q = quantize("z_q%d" % h, z_bf[:].rearrange("p c t -> p (c t)"), HALF)
+                pending = (clamped[:, t, :], lesser[:], fetched[2][:])
+            nc.vector.tensor_tensor(*pending, ALU.max)
+            z_bf, z_q = [], []
+            for a, b in MM_PIECES[h]:
+                piece = sbuf("z_bf%d" % a, [P, b - a, PACK], BF16)
+                nc.vector.tensor_tensor(
+                    piece[:].rearrange("p (c i) t -> p c t i", i=4),
+                    clamped[:, :, a - c0 : b - c0].rearrange("p t (c i) -> p c t i", i=4),
+                    gs_t[:].unsqueeze(1).unsqueeze(3).to_broadcast([P, (b - a) // 4, PACK, 4]),
+                    ALU.mult,
+                )
+                z_bf.append(piece)
+            for piece, (a, b) in zip(z_bf, MM_PIECES[h]):
+                z_q.append(quantize("z_q%d" % a, piece[:].rearrange("p c t -> p (c t)"), b - a))
             for t in range(PACK):
-                product(h_ps[t][:, half_cols(h)], (dk_words, dk_scales), t, z_q)
+                if h == 0:
+                    h_ps.append(ps.tile([P, S], F32, name="h_ps%d" % t, tag="bank%d" % t))
+                for q, (a, b) in zip(z_q, MM_PIECES[h]):
+                    product(h_ps[t][:, a:b], (dk_words, dk_scales), t, q, slice(0, b - a))
                 nc.vector.tensor_scalar(
-                    h_win[t][:, half_cols(h)],
-                    h_ps[t][:, half_cols(h)],
+                    h_win[t][:, c0:c1],
+                    h_ps[t][:, c0:c1],
                     0.0625,
-                    lows[0][t][:] if h == 1 else None,
+                    lows[0][:, t : t + 1] if h == 1 else None,
                     ALU.mult,
                     ALU.min,
-                    accum_out=lows[h][t][:],
+                    accum_out=lows[h][:, t : t + 1],
                 )
 
         out_rows = out.rearrange("(p t) c -> t p c", t=PACK)
+        pending = None
+
+        def finish(prod, t, h):
+            res = sbuf("res_%d_%d" % (t, h), [P, HALF], F32)
+            nc.vector.scalar_tensor_tensor(res[:], prod[:], -2.0, h_win[t][:, half_cols(h)], ALU.mult, ALU.add)
+            nc.sync.dma_start(out_rows[t][:, half_cols(h)], res[:])
+
         for t in range(PACK):
             bias = sbuf("bias%d" % t, [P, 1], F32)
-            nc.scalar.activation(bias[:], lows[1][t][:], ACT.Copy, scale=tau_t[:, t : t + 1])
+            nc.scalar.activation(bias[:], lows[1][:, t : t + 1], ACT.Copy, scale=tau_t[:, t : t + 1])
             for h in range(2):
                 ea = sbuf("ea_%d_%d" % (t, h), [P, HALF], F32)
                 nc.scalar.activation(
                     ea[:], h_win[t][:].indirect(half_list(n4_l, h)), ACT.Exp, bias=bias[:], scale=neg_tau[:, t : t + 1]
                 )
                 prod = sbuf("prod_%d_%d" % (t, h), [P, HALF], F32)
-                nc.vector.tensor_tensor(prod[:], h_win[t][:].indirect(half_list(n5_l, h)), ea[:], ALU.mult)
-                res = sbuf("res_%d_%d" % (t, h), [P, HALF], F32)
-                nc.vector.scalar_tensor_tensor(
-                    res[:], prod[:], -2.0, h_win[t][:, half_cols(h)], ALU.mult, ALU.add
-                )
-                nc.sync.dma_start(out_rows[t][:, half_cols(h)], res[:])
+                if (t, h) in N5_ON_SCALAR:
+                    h5 = sbuf("h5_%d_%d" % (t, h), [P, HALF], F32)
+                    nc.scalar.activation(h5[:], h_win[t][:].indirect(half_list(n5_l, h)), ACT.Copy)
+                    nc.vector.tensor_tensor(prod[:], h5[:], ea[:], ALU.mult)
+                else:
+                    nc.vector.tensor_tensor(prod[:], h_win[t][:].indirect(half_list(n5_l, h)), ea[:], ALU.mult)
+                if pending is not None:
+                    finish(*pending)
+                pending = (prod, t, h)
+        finish(*pending)

@@ -2,7 +2,7 @@ from contextlib import ExitStack
 
 import concourse.mybir as mybir
 
-FLOPS = 805306368
+FLOPS = 3 * 2 * 512 * 512 * 512
 
 F32 = mybir.dt.float32
 BF16 = mybir.dt.bfloat16
@@ -15,16 +15,15 @@ ALU = mybir.AluOpType
 ACT = mybir.ActivationFunctionType
 
 P = 128
-PACK = 4
+TILES = 4
 S = 512
-T = 1024
-G = 2048
+TOKENS = 1024
+CODEWORDS = 2048
+GROUP = 16
 HALF = S // 2
-CHUNKS = ((0, 256), (256, 512))
-MM_PIECES = (((0, 256),), ((256, 384), (384, 512)))
-Y_EVAC_ON_VECTOR = (1, 2)
-N5_ON_SCALAR = ((2, 1), (3, 0), (3, 1))
-LIST_COLS = S // 16
+QUARTER = S // 4
+CHUNKS = ((0, HALF), (HALF, HALF + QUARTER), (HALF + QUARTER, S))
+N5_ON_SCALAR = TILES - 1
 
 
 def tile_picked_twqclampbebz_none_p_kernel(
@@ -33,216 +32,231 @@ def tile_picked_twqclampbebz_none_p_kernel(
     nc = tc.nc
     with ExitStack() as ctx:
         sb = ctx.enter_context(tc.tile_pool(name="sb", bufs=1))
-        rot = ctx.enter_context(tc.tile_pool(name="rot", bufs=2))
         ps = ctx.enter_context(tc.psum_pool(name="ps", bufs=1))
 
-        def sbuf(name, shape, dtype, tag=None):
-            return sb.tile(shape, dtype, name=name, tag=tag or name, align_bytes=64)
+        def sbuf(name, shape, dtype, after=None):
+            return sb.tile(shape, dtype, name=name, tag=after or name, align_bytes=64)
 
-        def rotating(name, shape, dtype, tag):
-            return rot.tile(shape, dtype, name=name, tag=tag, align_bytes=64)
+        def half_cols(half):
+            return slice(half * HALF, (half + 1) * HALF)
+
+        def entries(lst, c0, c1):
+            return lst[:, c0 // GROUP : c1 // GROUP]
 
         def load_list(name, src):
-            lst = sbuf(name, [P, LIST_COLS], U16)
+            lst = sbuf(name, [P, S // GROUP], U16)
             nc.sync.dma_start(lst[:], src)
             return lst
 
-        def half_cols(h):
-            return slice(h * HALF, (h + 1) * HALF)
+        def load_words(name, src, columns):
+            table = sbuf(name, [P, columns], U32)
+            nc.sync.dma_start(table[:].bitcast(I32), src[0].rearrange("p n r -> p (n r)").bitcast(I32))
+            return table
 
-        def half_list(lst, h):
-            return lst[:, h * LIST_COLS // 2 : (h + 1) * LIST_COLS // 2]
+        def load_weight(name, w):
+            halves = []
+            for half in range(2):
+                raw = sbuf("%s%d" % (name, half), [P, TILES, HALF], F32)
+                nc.sync.dma_start(raw[:], w.rearrange("(p j) c -> p j c", j=TILES)[:, :, half_cols(half)])
+                halves.append(raw)
+            return halves
 
-        def load_weight_half(name, w, h):
-            raw = sbuf(name, [P, PACK, HALF], F32)
-            nc.sync.dma_start(raw[:], w.rearrange("(p j) c -> p j c", j=PACK)[:, :, half_cols(h)])
-            return raw
+        def load_by_row(name, vec):
+            by_row = sbuf(name, [P, TILES], F32)
+            nc.sync.dma_start(by_row[:], vec.rearrange("(p t) o -> p (t o)", t=TILES))
+            return by_row
 
-        xs_tab = sbuf("xs_tab", [P, T], U8)
-        ds_tab = sbuf("ds_tab", [P, G], U8)
-        nc.gpsimd.memset(xs_tab[:].bitcast(I32), 0)
-        nc.gpsimd.memset(ds_tab[:].bitcast(I32), 0)
+        xs_table = sbuf("xs_table", [P, TOKENS], U8)
+        ds_table = sbuf("ds_table", [P, CODEWORDS], U8)
+        nc.gpsimd.memset(xs_table[:].bitcast(I32), 0)
+        nc.gpsimd.memset(ds_table[:].bitcast(I32), 0)
 
         offs_l = load_list("offs_l", offs)
-        xw_tab = sbuf("xw_tab", [P, T], U32)
-        nc.sync.dma_start(xw_tab[:].bitcast(I32), x_words[0].rearrange("p n r -> p (n r)").bitcast(I32))
+        xw_table = load_words("xw_table", x_words, TOKENS)
         for q in range(4):
             nc.sync.dma_start(
-                xs_tab[:].bitcast(I32)[32 * q : 32 * q + 4, :], x_scales[0].bitcast(I32)[4 * q : 4 * q + 4, :]
+                xs_table[:].bitcast(I32)[32 * q : 32 * q + 4, :], x_scales[0].bitcast(I32)[4 * q : 4 * q + 4, :]
             )
         two_l = load_list("two_l", two)
-        w1_raw = [load_weight_half("w1_raw%d" % h, w1, h) for h in range(2)]
+        w1_raw = load_weight("w1_raw", w1)
+        w2_raw = load_weight("w2_raw", w2)
         n1_l = load_list("n1_l", n1)
         n2_l = load_list("n2_l", n2)
         n3_l = load_list("n3_l", n3)
-        w2_raw = [load_weight_half("w2_raw%d" % h, w2, h) for h in range(2)]
         k1_l = load_list("k1_l", k1)
+        dw_table = load_words("dw_table", d_words, CODEWORDS)
         for e in range(2):
-            nc.sync.dma_start(ds_tab[:].bitcast(I32)[e:P:16, :], d_scales[0].bitcast(I32)[e:16:2, :])
-        dw_tab = sbuf("dw_tab", [P, G], U32)
-        nc.sync.dma_start(dw_tab[:].bitcast(I32), d_words[0].rearrange("p n r -> p (n r)").bitcast(I32))
-        gs_t = sbuf("gs_t", [P, PACK], F32)
-        nc.sync.dma_start(gs_t[:], gs.rearrange("(p t) o -> p (t o)", t=PACK))
-        tau_t = sbuf("tau_t", [P, PACK], F32)
-        nc.sync.dma_start(tau_t[:], tau.rearrange("(p t) o -> p (t o)", t=PACK))
+            nc.sync.dma_start(ds_table[:].bitcast(I32)[e:P:GROUP, :], d_scales[0].bitcast(I32)[e:16:2, :])
+        gs_t = load_by_row("gs_t", gs)
+        tau_t = load_by_row("tau_t", tau)
         n4_l = load_list("n4_l", n4)
         n5_l = load_list("n5_l", n5)
 
-        def gather_packed(name, lst, scales_tag=None):
+        def round_weight(name, raw):
+            dealt = sbuf(name, [P, TILES, P, TILES], BF16)
+            for half in range(2):
+                nc.scalar.copy(
+                    dealt[:, :, half * P // 2 : (half + 1) * P // 2, :].rearrange("p t m j -> p m j t"),
+                    raw[half][:].rearrange("p j (m t) -> p m j t", t=TILES),
+                )
+            return dealt[:].rearrange("p t m j -> p (t m j)")
+
+        def pick_tokens(name, lst, scales_after=None):
             words = sbuf(name + "_words", [P, S], U32)
-            nc.vector.tensor_copy(words[:], xw_tab[:].indirect(lst[:]))
-            scales = sbuf(name + "_scales", [P, S], U8, tag=scales_tag)
-            nc.vector.tensor_copy(scales[:], xs_tab[:].indirect(lst[:]))
+            nc.vector.tensor_copy(words[:], xw_table[:].indirect(lst[:]))
+            scales = sbuf(name + "_scales", [P, S], U8, after=scales_after)
+            nc.vector.tensor_copy(scales[:], xs_table[:].indirect(lst[:]))
             return words, scales
 
-        def round_weight(name, raw):
-            dealt = sbuf(name, [P, PACK, P, PACK], BF16)
-            for h in range(2):
-                nc.scalar.copy(
-                    dealt[:, :, h * P // 2 : (h + 1) * P // 2, :].rearrange("p t m j -> p m j t"),
-                    raw[h][:].rearrange("p j (m t) -> p m j t", t=PACK),
-                )
-            return dealt
-
-        def quantize(name, values, width):
-            words = sbuf(name + "_words", [P, width], U32)
-            scales = sbuf(name + "_scales", [P, width], U8)
+        def quantize(name, values, columns):
+            words = sbuf(name + "_words", [P, columns], U32)
+            scales = sbuf(name + "_scales", [P, columns], U8)
             nc.vector.quantize_mx(out=words[:].bitcast(FP8X4), scales=scales[:], in_=values)
             return words, scales
 
-        def product(acc, stat, t, mov, mcols=slice(0, S)):
+        def product(acc, stationary, t, moving):
             cols = slice(t * P, (t + 1) * P)
             nc.tensor.matmul_mx(
                 out=acc,
-                lhsT=stat[0][:, cols].bitcast(FP8X4),
-                lhsT_scale=stat[1][:, cols],
-                rhs=mov[0][:, mcols].bitcast(FP8X4),
-                rhs_scale=mov[1][:, mcols],
+                lhsT=stationary[0][:, cols].bitcast(FP8X4),
+                lhsT_scale=stationary[1][:, cols],
+                rhs=moving[0][:].bitcast(FP8X4),
+                rhs_scale=moving[1][:],
                 start=True,
                 stop=True,
             )
 
         w1_bf = round_weight("w1_bf", w1_raw)
         w2_bf = round_weight("w2_bf", w2_raw)
-
-        xq = gather_packed("xq", offs_l)
-        w1_q = quantize("w1_q", w1_bf[:].rearrange("p t m j -> p (t m j)"), S)
-        x2 = gather_packed("x2", two_l, scales_tag="w1_bf")
-        y_ps, y_win = [], []
-        for t in range(PACK):
-            acc = ps.tile([P, S], F32, name="y_ps%d" % t)
-            product(acc[:], w1_q, t, xq)
-            y_ps.append(acc)
-            if t == 3:
-                continue
-            win = sbuf("y_win%d" % t, [P, S], F32, tag="w2_raw1" if t == 0 else None)
-            if t in Y_EVAC_ON_VECTOR:
-                nc.vector.tensor_copy(win[:], acc[:])
+        x_offs = pick_tokens("x_offs", offs_l)
+        w1_q = quantize("w1_q", w1_bf, S)
+        x_two = pick_tokens("x_two", two_l, scales_after="w1_bf")
+        w2_q = quantize("w2_q", w2_bf, S)
+        y_ps, y_sb, d_sb = [], [], []
+        for t in range(TILES):
+            y_ps.append(ps.tile([P, S], F32, name="y_ps%d" % t))
+            product(y_ps[t][:], w1_q, t, x_offs)
+            y_sb.append(sbuf("y_sb%d" % t, [P, S], F32))
+            if t == 0:
+                nc.scalar.copy(y_sb[t][:], y_ps[t][:])
             else:
-                nc.scalar.copy(win[:], acc[:])
-            y_win.append(win)
-        w2_q = quantize("w2_q", w2_bf[:].rearrange("p t m j -> p (t m j)"), S)
-        d_ps, d_win = [], []
-        for t in range(PACK):
-            acc = ps.tile([P, S], F32, name="d_ps%d" % t, tag="bank%d" % t)
-            product(acc[:], w2_q, t, x2)
-            d_ps.append(acc)
-            d_win.append(sbuf("d_win%d" % t, [P, S], F32))
+                nc.vector.tensor_copy(y_sb[t][:], y_ps[t][:])
+        for t in range(TILES):
+            d_ps = ps.tile([P, S], F32, name="d_ps%d" % t)
+            product(d_ps[:], w2_q, t, x_two)
+            d_sb.append(sbuf("d_sb%d" % t, [P, S], F32))
+            nc.vector.tensor_copy(d_sb[t][:], d_ps[:])
 
-        dk_bytes = rotating("dk_bytes", [P, S], U8, "lesser")
-        nc.vector.tensor_copy(dk_bytes[:], ds_tab[:].indirect(k1_l[:]))
+        dk_bytes = sbuf("dk_bytes", [P, S], U8)
+        nc.vector.tensor_copy(dk_bytes[:], ds_table[:].indirect(k1_l[:]))
         dk_scales = sbuf("dk_scales", [P, S], U8)
         nc.vector.tensor_copy(
-            dk_scales[:].rearrange("p (t m) -> p m t", t=PACK), dk_bytes[:].rearrange("p (m t) -> p m t", t=PACK)
+            dk_scales[:].rearrange("p (t m) -> p m t", t=TILES), dk_bytes[:].rearrange("p (m t) -> p m t", t=TILES)
         )
         for e in range(2):
             nc.sync.dma_start(dk_scales[:].bitcast(I32)[2 + e : P : 32, :], dk_scales[:].bitcast(I32)[16 + e : P : 32, :])
-        dk_picked = rotating("dk_picked", [P, S], U32, "lesser")
-        nc.vector.tensor_copy(dk_picked[:], dw_tab[:].indirect(k1_l[:]))
+        dk_picked = sbuf("dk_picked", [P, S], U32)
+        nc.vector.tensor_copy(dk_picked[:], dw_table[:].indirect(k1_l[:]))
         dk_words = sbuf("dk_words", [P, S], U32)
         nc.vector.tensor_copy(
-            dk_words[:].rearrange("p (t m) -> p m t", t=PACK), dk_picked[:].rearrange("p (m t) -> p m t", t=PACK)
+            dk_words[:].rearrange("p (t m) -> p m t", t=TILES), dk_picked[:].rearrange("p (m t) -> p m t", t=TILES)
         )
-        neg_tau = sbuf("neg_tau", [P, PACK], F32)
-        nc.vector.tensor_scalar(neg_tau[:], tau_t[:], -1.0, None, ALU.mult)
+        neg_tau = sbuf("neg_tau", [P, TILES], F32)
+        nc.gpsimd.tensor_scalar(neg_tau[:], tau_t[:], -1.0, 0.0, ALU.mult, ALU.add)
 
-        h_ps = []
-        h_win = [sbuf("h_win%d" % t, [P, S], F32) for t in range(PACK)]
-        lows = [sbuf("low%d" % h, [P, PACK], F32) for h in range(2)]
-        for h, (c0, c1) in enumerate(CHUNKS):
-            width = c1 - c0
-            clamped = sbuf("clamped%d" % h, [P, PACK, width], F32)
-            pending = None
-            for t in range(PACK):
-                if h == 0:
-                    if t == 3:
-                        y_win.append(sbuf("y_win3", [P, S], F32, tag="w2_bf"))
-                        nc.scalar.copy(y_win[3][:], y_ps[3][:])
-                    nc.scalar.copy(d_win[t][:], d_ps[t][:])
-                fetched = []
-                for nm, win, lst in (("y1", y_win[t], n1_l), ("d2", d_win[t], n2_l), ("d3", d_win[t], n3_l)):
-                    got = sbuf("%s_%d_%d" % (nm, h, t), [P, width], F32, tag="%s_%d" % (nm, t))
-                    nc.scalar.activation(got[:], win[:].indirect(lst[:, c0 // 16 : c1 // 16]), ACT.Copy)
-                    fetched.append(got)
-                diff = rotating("diff_%d_%d" % (h, t), [P, width], F32, "diff")
-                nc.vector.scalar_tensor_tensor(diff[:], fetched[0][:], -0.5, y_ps[t][:, c0:c1], ALU.mult, ALU.add)
-                if pending is not None:
-                    nc.vector.tensor_tensor(*pending, ALU.max)
-                lesser = rotating("lesser_%d_%d" % (h, t), [P, width], F32, "lesser")
-                nc.vector.tensor_tensor(lesser[:], diff[:], fetched[1][:], ALU.min)
-                pending = (clamped[:, t, :], lesser[:], fetched[2][:])
-            nc.vector.tensor_tensor(*pending, ALU.max)
-            z_bf, z_q = [], []
-            for a, b in MM_PIECES[h]:
-                piece = sbuf("z_bf%d" % a, [P, b - a, PACK], BF16)
-                nc.vector.tensor_tensor(
-                    piece[:].rearrange("p (c i) t -> p c t i", i=4),
-                    clamped[:, :, a - c0 : b - c0].rearrange("p t (c i) -> p c t i", i=4),
-                    gs_t[:].unsqueeze(1).unsqueeze(3).to_broadcast([P, (b - a) // 4, PACK, 4]),
-                    ALU.mult,
+        def difference(half):
+            y_n1 = sbuf("y_n1_%d" % half, [P, TILES, HALF], F32, after="ds_table" if half else None)
+            pairs = [
+                sbuf("diff%d_%d" % (half, pair), [P, 2, HALF], F32, after=("d_n2_1", "d_n3_1")[pair] if half else None)
+                for pair in range(2)
+            ]
+            for t in range(TILES):
+                picked = y_sb[t][:].indirect(entries(n1_l, half * HALF, (half + 1) * HALF))
+                if half == 0:
+                    nc.scalar.activation(y_n1[:, t, :], picked, ACT.Copy, scale=-0.5)
+                    nc.gpsimd.tensor_tensor(pairs[t // 2][:, t % 2, :], y_n1[:, t, :], y_sb[t][:, half_cols(half)], ALU.add)
+                else:
+                    nc.scalar.activation(y_n1[:, t, :], picked, ACT.Copy)
+                    nc.vector.scalar_tensor_tensor(
+                        pairs[t // 2][:, t % 2, :], y_n1[:, t, :], -0.5, y_ps[t][:, half_cols(half)], ALU.mult, ALU.add
+                    )
+            return pairs
+
+        h_ps = {}
+        for k, (c0, c1) in enumerate(CHUNKS):
+            width, half, start = c1 - c0, c0 // HALF, c0 % HALF
+            if start == 0:
+                diff = difference(half)
+                if half == 1:
+                    d_late = sbuf("d_late", [P, 2, 2, TILES, QUARTER], F32, after="dw_table")
+            clamped = sbuf("clamped%d" % k, [P, TILES, width], F32)
+            for pair in range(2):
+                both = slice(2 * pair, 2 * pair + 2)
+                if half == 0:
+                    d_n2 = sbuf("d_n2_%d" % pair, [P, 2, width], F32)[:]
+                    d_n3 = sbuf("d_n3_%d" % pair, [P, 2, width], F32)[:]
+                else:
+                    d_n2, d_n3 = d_late[:, k - 1, 0, both, :], d_late[:, k - 1, 1, both, :]
+                for t in (2 * pair, 2 * pair + 1):
+                    for fetched, lst in ((d_n2, n2_l), (d_n3, n3_l)):
+                        nc.scalar.activation(fetched[:, t % 2, :], d_sb[t][:].indirect(entries(lst, c0, c1)), ACT.Copy)
+                lesser = sbuf(
+                    "lesser%d_%d" % (k, pair), [P, 2, width], F32, after=None if k else ("dk_bytes", "dk_picked")[pair]
                 )
-                z_bf.append(piece)
-            for piece, (a, b) in zip(z_bf, MM_PIECES[h]):
-                z_q.append(quantize("z_q%d" % a, piece[:].rearrange("p c t -> p (c t)"), b - a))
-            for t in range(PACK):
-                if h == 0:
-                    h_ps.append(ps.tile([P, S], F32, name="h_ps%d" % t, tag="bank%d" % t))
-                for q, (a, b) in zip(z_q, MM_PIECES[h]):
-                    product(h_ps[t][:, a:b], (dk_words, dk_scales), t, q, slice(0, b - a))
+                nc.vector.tensor_tensor(lesser[:], diff[pair][:, :, start : start + width], d_n2, ALU.min)
+                nc.vector.tensor_tensor(clamped[:, both, :], lesser[:], d_n3, ALU.max)
+            z_bf = sbuf("z_bf%d" % k, [P, width, TILES], BF16)
+            nc.vector.tensor_tensor(
+                z_bf[:].rearrange("p (c i) t -> p c t i", i=4),
+                clamped[:].rearrange("p t (c i) -> p c t i", i=4),
+                gs_t[:].unsqueeze(1).unsqueeze(3).to_broadcast([P, width // 4, TILES, 4]),
+                ALU.mult,
+            )
+            z_q = quantize("z_q%d" % k, z_bf[:].rearrange("p c t -> p (c t)"), width)
+            for t in range(TILES):
+                if start == 0:
+                    h_ps[t, half] = ps.tile([P, HALF], F32, name="h_ps%d_%d" % (t, half), tag=("d_ps%d", "y_ps%d")[half] % t)
+                product(h_ps[t, half][:, start : start + width], (dk_words, dk_scales), t, z_q)
+
+        h_sb = [sbuf("h_sb%d" % t, [P, S], F32) for t in range(TILES)]
+        low = [sbuf("low%d" % half, [P, TILES], F32) for half in range(2)]
+        for half in range(2):
+            for t in range(TILES):
                 nc.vector.tensor_scalar(
-                    h_win[t][:, c0:c1],
-                    h_ps[t][:, c0:c1],
+                    h_sb[t][:, half_cols(half)],
+                    h_ps[t, half][:],
                     0.0625,
-                    lows[0][:, t : t + 1] if h == 1 else None,
+                    low[0][:, t : t + 1] if half else None,
                     ALU.mult,
                     ALU.min,
-                    accum_out=lows[h][:, t : t + 1],
+                    accum_out=low[half][:, t : t + 1],
                 )
 
-        out_rows = out.rearrange("(p t) c -> t p c", t=PACK)
+        out_rows = out.rearrange("(p t) c -> t p c", t=TILES)
+
+        def finish(weighted, t, half):
+            result = sbuf("result%d_%d" % (t, half), [P, HALF], F32)
+            nc.vector.scalar_tensor_tensor(result[:], weighted[:], -2.0, h_sb[t][:, half_cols(half)], ALU.mult, ALU.add)
+            nc.sync.dma_start(out_rows[t][:, half_cols(half)], result[:])
+
         pending = None
-
-        def finish(prod, t, h):
-            res = sbuf("res_%d_%d" % (t, h), [P, HALF], F32)
-            nc.vector.scalar_tensor_tensor(res[:], prod[:], -2.0, h_win[t][:, half_cols(h)], ALU.mult, ALU.add)
-            nc.sync.dma_start(out_rows[t][:, half_cols(h)], res[:])
-
-        for t in range(PACK):
+        for t in range(TILES):
             bias = sbuf("bias%d" % t, [P, 1], F32)
-            nc.scalar.activation(bias[:], lows[1][:, t : t + 1], ACT.Copy, scale=tau_t[:, t : t + 1])
-            for h in range(2):
-                ea = sbuf("ea_%d_%d" % (t, h), [P, HALF], F32)
+            nc.scalar.activation(bias[:], low[1][:, t : t + 1], ACT.Copy, scale=tau_t[:, t : t + 1])
+            for half in range(2):
+                c0, c1 = half * HALF, (half + 1) * HALF
+                ea = sbuf("ea%d_%d" % (t, half), [P, HALF], F32)
                 nc.scalar.activation(
-                    ea[:], h_win[t][:].indirect(half_list(n4_l, h)), ACT.Exp, bias=bias[:], scale=neg_tau[:, t : t + 1]
+                    ea[:], h_sb[t][:].indirect(entries(n4_l, c0, c1)), ACT.Exp, bias=bias[:], scale=neg_tau[:, t : t + 1]
                 )
-                prod = sbuf("prod_%d_%d" % (t, h), [P, HALF], F32)
-                if (t, h) in N5_ON_SCALAR:
-                    h5 = sbuf("h5_%d_%d" % (t, h), [P, HALF], F32)
-                    nc.scalar.activation(h5[:], h_win[t][:].indirect(half_list(n5_l, h)), ACT.Copy)
-                    nc.vector.tensor_tensor(prod[:], h5[:], ea[:], ALU.mult)
+                weighted = sbuf("weighted%d_%d" % (t, half), [P, HALF], F32)
+                if t == N5_ON_SCALAR:
+                    h_n5 = sbuf("h_n5_%d" % half, [P, HALF], F32)
+                    nc.scalar.activation(h_n5[:], h_sb[t][:].indirect(entries(n5_l, c0, c1)), ACT.Copy)
+                    nc.vector.tensor_tensor(weighted[:], h_n5[:], ea[:], ALU.mult)
                 else:
-                    nc.vector.tensor_tensor(prod[:], h_win[t][:].indirect(half_list(n5_l, h)), ea[:], ALU.mult)
+                    nc.vector.tensor_tensor(weighted[:], h_sb[t][:].indirect(entries(n5_l, c0, c1)), ea[:], ALU.mult)
                 if pending is not None:
                     finish(*pending)
-                pending = (prod, t, h)
+                pending = (weighted, t, half)
         finish(*pending)

@@ -197,8 +197,8 @@ def tile_picked_twqclampbebz_none_p_kernel(
                     d_n3 = sbuf("d_n3_%d" % pair, [P, 2, width], F32)[:]
                 else:
                     d_n2, d_n3 = d_late[:, k - 1, 0, both, :], d_late[:, k - 1, 1, both, :]
-                for t in (2 * pair, 2 * pair + 1):
-                    for fetched, lst in ((d_n2, n2_l), (d_n3, n3_l)):
+                for fetched, lst in ((d_n2, n2_l), (d_n3, n3_l)):
+                    for t in (2 * pair, 2 * pair + 1):
                         nc.scalar.activation(fetched[:, t % 2, :], d_sb[t][:].indirect(entries(lst, c0, c1)), ACT.Copy)
                 lesser = sbuf(
                     "lesser%d_%d" % (k, pair), [P, 2, width], F32, after=None if k else ("dk_bytes", "dk_picked")[pair]

from contextlib import ExitStack

import concourse.mybir as mybir

FLOPS = 3 * 2 * 512 * 512 * 512

F32 = mybir.dt.float32
BF16 = mybir.dt.bfloat16
I32 = mybir.dt.int32
U32 = mybir.dt.uint32
U16 = mybir.dt.uint16
U8 = mybir.dt.uint8
FP8X4 = mybir.dt.float8_e4m3fn_x4
ALU = mybir.AluOpType
ACT = mybir.ActivationFunctionType

P = 128
TILES = 4
S = 512
TOKENS = 1024
CODEWORDS = 2048
GROUP = 16
HALF = S // 2
QUARTER = S // 4
CHUNKS = ((0, HALF), (HALF, HALF + QUARTER), (HALF + QUARTER, S))
N5_ON_SCALAR = TILES - 1


def tile_picked_twqclampbebz_none_p_kernel(
    tc, x_words, x_scales, w1, w2, gs, d_words, d_scales, tau, offs, two, n1, n2, n3, k1, n4, n5, out
):
    nc = tc.nc
    with ExitStack() as ctx:
        sb = ctx.enter_context(tc.tile_pool(name="sb", bufs=1))
        ps = ctx.enter_context(tc.psum_pool(name="ps", bufs=1))

        def sbuf(name, shape, dtype, after=None):
            return sb.tile(shape, dtype, name=name, tag=after or name, align_bytes=64)

        def half_cols(half):
            return slice(half * HALF, (half + 1) * HALF)

        def entries(lst, c0, c1):
            return lst[:, c0 // GROUP : c1 // GROUP]

        def load_list(name, src):
            lst = sbuf(name, [P, S // GROUP], U16)
            nc.sync.dma_start(lst[:], src)
            return lst

        def load_words(name, src, columns):
            table = sbuf(name, [P, columns], U32)
            nc.sync.dma_start(table[:].bitcast(I32), src[0].rearrange("p n r -> p (n r)").bitcast(I32))
            return table

        def load_weight(name, w):
            halves = []
            for half in range(2):
                raw = sbuf("%s%d" % (name, half), [P, TILES, HALF], F32)
                nc.sync.dma_start(raw[:], w.rearrange("(p j) c -> p j c", j=TILES)[:, :, half_cols(half)])
                halves.append(raw)
            return halves

        def load_by_row(name, vec):
            by_row = sbuf(name, [P, TILES], F32)
            nc.sync.dma_start(by_row[:], vec.rearrange("(p t) o -> p (t o)", t=TILES))
            return by_row

        xs_table = sbuf("xs_table", [P, TOKENS], U8)
        ds_table = sbuf("ds_table", [P, CODEWORDS], U8)
        nc.gpsimd.memset(xs_table[:].bitcast(I32), 0)
        nc.gpsimd.memset(ds_table[:].bitcast(I32), 0)

        offs_l = load_list("offs_l", offs)
        xw_table = load_words("xw_table", x_words, TOKENS)
        for q in range(4):
            nc.sync.dma_start(
                xs_table[:].bitcast(I32)[32 * q : 32 * q + 4, :], x_scales[0].bitcast(I32)[4 * q : 4 * q + 4, :]
            )
        two_l = load_list("two_l", two)
        w1_raw = load_weight("w1_raw", w1)
        w2_raw = load_weight("w2_raw", w2)
        n1_l = load_list("n1_l", n1)
        n2_l = load_list("n2_l", n2)
        n3_l = load_list("n3_l", n3)
        k1_l = load_list("k1_l", k1)
        dw_table = load_words("dw_table", d_words, CODEWORDS)
        for e in range(2):
            nc.sync.dma_start(ds_table[:].bitcast(I32)[e:P:GROUP, :], d_scales[0].bitcast(I32)[e:16:2, :])
        gs_t = load_by_row("gs_t", gs)
        tau_t = load_by_row("tau_t", tau)
        n4_l = load_list("n4_l", n4)
        n5_l = load_list("n5_l", n5)

        def round_weight(name, raw):
            dealt = sbuf(name, [P, TILES, P, TILES], BF16)
            for half in range(2):
                nc.scalar.copy(
                    dealt[:, :, half * P // 2 : (half + 1) * P // 2, :].rearrange("p t m j -> p m j t"),
                    raw[half][:].rearrange("p j (m t) -> p m j t", t=TILES),
                )
            return dealt[:].rearrange("p t m j -> p (t m j)")

        def pick_tokens(name, lst, scales_after=None):
            words = sbuf(name + "_words", [P, S], U32)
            nc.vector.tensor_copy(words[:], xw_table[:].indirect(lst[:]))
            scales = sbuf(name + "_scales", [P, S], U8, after=scales_after)
            nc.vector.tensor_copy(scales[:], xs_table[:].indirect(lst[:]))
            return words, scales

        def quantize(name, values, columns):
            words = sbuf(name + "_words", [P, columns], U32)
            scales = sbuf(name + "_scales", [P, columns], U8)
            nc.vector.quantize_mx(out=words[:].bitcast(FP8X4), scales=scales[:], in_=values)
            return words, scales

        def product(acc, stationary, t, moving):
            cols = slice(t * P, (t + 1) * P)
            nc.tensor.matmul_mx(
                out=acc,
                lhsT=stationary[0][:, cols].bitcast(FP8X4),
                lhsT_scale=stationary[1][:, cols],
                rhs=moving[0][:].bitcast(FP8X4),
                rhs_scale=moving[1][:],
                start=True,
                stop=True,
            )

        w1_bf = round_weight("w1_bf", w1_raw)
        w2_bf = round_weight("w2_bf", w2_raw)
        x_offs = pick_tokens("x_offs", offs_l)
        w1_q = quantize("w1_q", w1_bf, S)
        x_two = pick_tokens("x_two", two_l, scales_after="w1_bf")
        w2_q = quantize("w2_q", w2_bf, S)
        y_ps, y_sb, d_sb = [], [], []
        for t in range(TILES):
            y_ps.append(ps.tile([P, S], F32, name="y_ps%d" % t))
            product(y_ps[t][:], w1_q, t, x_offs)
            y_sb.append(sbuf("y_sb%d" % t, [P, S], F32))
            if t == 0:
                nc.scalar.copy(y_sb[t][:], y_ps[t][:])
            else:
                nc.vector.tensor_copy(y_sb[t][:], y_ps[t][:])
        for t in range(TILES):
            d_ps = ps.tile([P, S], F32, name="d_ps%d" % t)
            product(d_ps[:], w2_q, t, x_two)
            d_sb.append(sbuf("d_sb%d" % t, [P, S], F32))
            nc.vector.tensor_copy(d_sb[t][:], d_ps[:])

        dk_bytes = sbuf("dk_bytes", [P, S], U8)
        nc.vector.tensor_copy(dk_bytes[:], ds_table[:].indirect(k1_l[:]))
        dk_scales = sbuf("dk_scales", [P, S], U8)
        nc.vector.tensor_copy(
            dk_scales[:].rearrange("p (t m) -> p m t", t=TILES), dk_bytes[:].rearrange("p (m t) -> p m t", t=TILES)
        )
        for e in range(2):
            nc.sync.dma_start(dk_scales[:].bitcast(I32)[2 + e : P : 32, :], dk_scales[:].bitcast(I32)[16 + e : P : 32, :])
        dk_picked = sbuf("dk_picked", [P, S], U32)
        nc.vector.tensor_copy(dk_picked[:], dw_table[:].indirect(k1_l[:]))
        dk_words = sbuf("dk_words", [P, S], U32)
        nc.vector.tensor_copy(
            dk_words[:].rearrange("p (t m) -> p m t", t=TILES), dk_picked[:].rearrange("p (m t) -> p m t", t=TILES)
        )
        neg_tau = sbuf("neg_tau", [P, TILES], F32)
        nc.gpsimd.tensor_scalar(neg_tau[:], tau_t[:], -1.0, 0.0, ALU.mult, ALU.add)

        def difference(half):
            y_n1 = sbuf("y_n1_%d" % half, [P, TILES, HALF], F32, after="ds_table" if half else None)
            pairs = [
                sbuf("diff%d_%d" % (half, pair), [P, 2, HALF], F32, after=("d_n2_1", "d_n3_1")[pair] if half else None)
                for pair in range(2)
            ]
            for t in range(TILES):
                picked = y_sb[t][:].indirect(entries(n1_l, half * HALF, (half + 1) * HALF))
                if half == 0:
                    nc.scalar.activation(y_n1[:, t, :], picked, ACT.Copy, scale=-0.5)
                    nc.gpsimd.tensor_tensor(pairs[t // 2][:, t % 2, :], y_n1[:, t, :], y_sb[t][:, half_cols(half)], ALU.add)
                else:
                    nc.scalar.activation(y_n1[:, t, :], picked, ACT.Copy)
                    nc.vector.scalar_tensor_tensor(
                        pairs[t // 2][:, t % 2, :], y_n1[:, t, :], -0.5, y_ps[t][:, half_cols(half)], ALU.mult, ALU.add
                    )
            return pairs

        h_ps = {}
        for k, (c0, c1) in enumerate(CHUNKS):
            width, half, start = c1 - c0, c0 // HALF, c0 % HALF
            if start == 0:
                diff = difference(half)
                if half == 1:
                    d_late = sbuf("d_late", [P, 2, 2, TILES, QUARTER], F32, after="dw_table")
            clamped = sbuf("clamped%d" % k, [P, TILES, width], F32)
            for pair in range(2):
                both = slice(2 * pair, 2 * pair + 2)
                if half == 0:
                    d_n2 = sbuf("d_n2_%d" % pair, [P, 2, width], F32)[:]
                    d_n3 = sbuf("d_n3_%d" % pair, [P, 2, width], F32)[:]
                else:
                    d_n2, d_n3 = d_late[:, k - 1, 0, both, :], d_late[:, k - 1, 1, both, :]
                for fetched, lst in ((d_n2, n2_l), (d_n3, n3_l)):
                    for t in (2 * pair, 2 * pair + 1):
                        nc.scalar.activation(fetched[:, t % 2, :], d_sb[t][:].indirect(entries(lst, c0, c1)), ACT.Copy)
                lesser = sbuf(
                    "lesser%d_%d" % (k, pair), [P, 2, width], F32, after=None if k else ("dk_bytes", "dk_picked")[pair]
                )
                nc.vector.tensor_tensor(lesser[:], diff[pair][:, :, start : start + width], d_n2, ALU.min)
                nc.vector.tensor_tensor(clamped[:, both, :], lesser[:], d_n3, ALU.max)
            z_bf = sbuf("z_bf%d" % k, [P, width, TILES], BF16)
            nc.vector.tensor_tensor(
                z_bf[:].rearrange("p (c i) t -> p c t i", i=4),
                clamped[:].rearrange("p t (c i) -> p c t i", i=4),
                gs_t[:].unsqueeze(1).unsqueeze(3).to_broadcast([P, width // 4, TILES, 4]),
                ALU.mult,
            )
            z_q = quantize("z_q%d" % k, z_bf[:].rearrange("p c t -> p (c t)"), width)
            for t in range(TILES):
                if start == 0:
                    h_ps[t, half] = ps.tile([P, HALF], F32, name="h_ps%d_%d" % (t, half), tag=("d_ps%d", "y_ps%d")[half] % t)
                product(h_ps[t, half][:, start : start + width], (dk_words, dk_scales), t, z_q)

        h_sb = [sbuf("h_sb%d" % t, [P, S], F32) for t in range(TILES)]
        low = [sbuf("low%d" % half, [P, TILES], F32) for half in range(2)]
        for half in range(2):
            for t in range(TILES):
                nc.vector.tensor_scalar(
                    h_sb[t][:, half_cols(half)],
                    h_ps[t, half][:],
                    0.0625,
                    low[0][:, t : t + 1] if half else None,
                    ALU.mult,
                    ALU.min,
                    accum_out=low[half][:, t : t + 1],
                )

        out_rows = out.rearrange("(p t) c -> t p c", t=TILES)

        def finish(weighted, t, half):
            result = sbuf("result%d_%d" % (t, half), [P, HALF], F32)
            nc.vector.scalar_tensor_tensor(result[:], weighted[:], -2.0, h_sb[t][:, half_cols(half)], ALU.mult, ALU.add)
            nc.sync.dma_start(out_rows[t][:, half_cols(half)], result[:])

        pending = None
        for t in range(TILES):
            bias = sbuf("bias%d" % t, [P, 1], F32)
            nc.scalar.activation(bias[:], low[1][:, t : t + 1], ACT.Copy, scale=tau_t[:, t : t + 1])
            for half in range(2):
                c0, c1 = half * HALF, (half + 1) * HALF
                ea = sbuf("ea%d_%d" % (t, half), [P, HALF], F32)
                nc.scalar.activation(
                    ea[:], h_sb[t][:].indirect(entries(n4_l, c0, c1)), ACT.Exp, bias=bias[:], scale=neg_tau[:, t : t + 1]
                )
                weighted = sbuf("weighted%d_%d" % (t, half), [P, HALF], F32)
                if t == N5_ON_SCALAR:
                    h_n5 = sbuf("h_n5_%d" % half, [P, HALF], F32)
                    nc.scalar.activation(h_n5[:], h_sb[t][:].indirect(entries(n5_l, c0, c1)), ACT.Copy)
                    nc.vector.tensor_tensor(weighted[:], h_n5[:], ea[:], ALU.mult)
                else:
                    nc.vector.tensor_tensor(weighted[:], h_sb[t][:].indirect(entries(n5_l, c0, c1)), ea[:], ALU.mult)
                if pending is not None:
                    finish(*pending)
                pending = (weighted, t, half)
        finish(*pending)
